import numpy as np
CORES = [0,1,8,9,16,17,24,25,32,33,40,41,48,49,56,57,64,65,72,73,80,81,88,89,96,97,104,105,112,113,120,121,128,129,136,137,144,145,152,153,160,161,168,169,176,177,184,185,192,193,200,201,208,209,216,217,224,225,232,233,240,241,248,249,256,257,264,265,272,273,280,281,288,289,296,297,304,305,312,313,320,321,328,329,336,337,344,345,352,353,360,361,368,369,376,377,384,385,392,393,400,401,408,409,416,417,424,425,432,433,440,441,448,449,456,457,464,465,472,473,480,481,488,489,496,497,504,505]
N = 128
ROUNDS = 8
PERM = [[i, (i + 64) % N] for i in range(N)]
def setup_inputs(rng):
    return {"x": rng.standard_normal((N, ROUNDS, 128, 64), dtype=np.float32)}
def reference(x):
    y = np.empty_like(x)
    for s, d in PERM:
        y[d] = x[s]
    return {"y": y}

from concourse.bass import DstId, RemoteDMATransfer

BATCHES = 4

SCRATCH = {
    "buf": ("dram", [2, 128, 64], "float32"),
}
SEMAPHORES = ["moved", "sent", "arrived"]

HALF = (0x0F, 0xF0)
ONE = (0x01, 0x02)


def rank_program(g, core, T, topo):
    if T.rank_of(core) is None:
        return
    me = topo.host(core)
    count = {"moved": 0, "sent": 0, "arrived": 0}

    def peer(h):
        return h * 128 + core % 128

    def dst_id(h):
        rid, pid = topo.addr(peer(h), core)
        return DstId(rid=rid, pnc=pid)

    def local_copy(out, in_):
        g.dma_start(out, in_).then_inc(T.sem.moved, 16)
        count["moved"] += 16
        g.wait_ge(T.sem.moved, count["moved"])

    def send_pair(pieces):
        g.remote_dma_fused(
            [
                RemoteDMATransfer(dst_ids=[dst_id(h)], dma_engine_mask=HALF[i], remote_sem=T.sem.arrived,
                                  src=T.buf[mine], dst=T.buf[its])
                for i, (mine, h, its) in enumerate(pieces)
            ],
            local_sem=T.sem.sent,
        )
        count["sent"] += 8

    def await_pair():
        count["arrived"] += 8
        g.wait_ge(T.sem.arrived, count["arrived"])

    def await_sent():
        g.wait_ge(T.sem.sent, count["sent"])

    def stage(j):
        local_copy(T.buf[:], T.x[2 * j:2 * j + 2])

    def originate(staged_first):
        passer = (1, 3) if me % 2 == 0 else (0, 2)
        for j in range(BATCHES):
            if j > 0 or not staged_first:
                stage(j)
            land = (j + me // 2) % 2
            send_pair([(s, passer[s], land) for s in (0, 1)])
            await_sent()
            await_pair()
            local_copy(T.y[2 * j:2 * j + 2], T.buf[:])

    def pass_on():
        serve = me // 2
        for j in range(BATCHES):
            await_pair()
            send_pair([((j + o // 2) % 2, (o + 2) % 4, serve) for o in (1 - me % 2, 3 - me % 2)])
        await_sent()

    if me % 2 == 0:
        originate(False)
        g.remote_dma_fused(
            [
                RemoteDMATransfer(dst_ids=[dst_id(h)], dma_engine_mask=ONE[i], remote_sem=T.sem.arrived)
                for i, h in enumerate((1, 3))
            ],
            local_sem=T.sem.sent,
        )
        count["sent"] += 2
        pass_on()
    else:
        pass_on()
        stage(0)
        count["arrived"] += 2
        g.wait_ge(T.sem.arrived, count["arrived"])
        originate(True)
